import numpy as np
import ml_dtypes


def mxq(x, axis, fmt="e4m3"):
    dtype, down = {"e4m3": (ml_dtypes.float8_e4m3fn, 7), "e5m2": (ml_dtypes.float8_e5m2, 14)}[fmt]
    v = np.moveaxis(np.asarray(x, np.float32).astype(ml_dtypes.bfloat16).astype(np.float64), axis, -1)
    blocks = v.reshape(v.shape[:-1] + (-1, 32))
    amax = np.abs(blocks).max(-1, keepdims=True)
    byte = np.maximum(np.where(amax > 0, np.frexp(amax)[1] - 1 + 127, 0) - down, 1)
    scale = np.exp2(byte - 127.0)
    codes = (blocks / scale).astype(np.float32).astype(dtype).astype(np.float64)
    return np.moveaxis((codes * scale).reshape(v.shape), -1, axis)


WIDE = False


def mx_kscale(k):
    if not WIDE:
        return np.ones(k)
    levels = np.array([10, -10, 5, -5, 0])
    if k % 512:
        return np.exp2(np.random.permutation(np.resize(levels, k // 32))).repeat(32)
    a = np.empty((k // 512, 16))
    for p in range(k // 512):
        a[p, :8] = np.random.permutation(np.resize(levels, 8))
        for g in range(8):
            far = levels[np.abs(levels - a[p, g]) >= 10]
            a[p, g + 8] = far[np.random.randint(len(far))]
    return np.exp2(a.ravel()).repeat(32)


def f64(x):
    return np.asarray(x).astype(np.float64)


def striped(idx):
    return np.tile(np.asarray(idx).reshape(-1, 16).T, (8, 1)).astype(np.uint16)


def unstriped(offs):
    return offs[:16].T.reshape(-1).astype(np.int64)


E2M1 = np.array([0.0, 0.5, 1.0, 1.5, 2.0, 3.0, 4.0, 6.0, -0.0, -0.5, -1.0, -1.5, -2.0, -3.0, -4.0, -6.0])


def pack_weight(w, fmt):
    k, n = w.shape
    w = f64(np.asarray(w, np.float32).astype(ml_dtypes.bfloat16)).reshape(k // 32, 32, n)
    amax = np.abs(w).max(1)
    if fmt == "e4m3":
        byte = np.frexp(amax)[1] - 1 + 127 - 7
    else:
        mant, ex = np.frexp(amax / 6.0)
        byte = np.where(mant > 0.5, ex, ex - 1) + 127
    byte = np.clip(np.where(amax > 0, byte, 1), 1, 254)
    scaled = (w * np.exp2(127.0 - byte)[:, None, :]).reshape(k, n).astype(np.float32)
    by_word = np.ascontiguousarray(scaled.reshape(k // 512, 128, 4, n).transpose(0, 1, 3, 2))
    if fmt == "e4m3":
        words = by_word.astype(ml_dtypes.float8_e4m3fn).view(np.uint8)
    else:
        c = by_word.astype(ml_dtypes.float4_e2m1fn).view(np.uint8) & 0xF
        words = (c[..., 0::2] | (c[..., 1::2] << 4)).reshape(k // 512, 128, 2 * n)
    return np.ascontiguousarray(words), np.ascontiguousarray(byte.astype(np.uint8).reshape(k // 512, 16, n))


def unpack_weight(words, scales, fmt):
    g, _, n = scales.shape
    words = np.ascontiguousarray(words).reshape(g, 128, n, -1)
    if fmt == "e4m3":
        vals = words.view(ml_dtypes.float8_e4m3fn).astype(np.float64)
    else:
        nib = np.empty((g, 128, n, 4), np.uint8)
        nib[..., 0::2] = words & 0xF
        nib[..., 1::2] = words >> 4
        vals = E2M1[nib]
    vals = vals * np.repeat(np.exp2(scales.astype(np.float64) - 127.0), 8, axis=1)[..., None]
    return vals.transpose(0, 1, 3, 2).reshape(g * 512, n)


def sigmoid(v):
    return 1.0 / (1.0 + np.exp(-v))


D, T, I, Q, E, M = 512, 2048, 512, 512, 512, 1024


def setup_inputs():
    n = np.random.standard_normal
    idx = np.random.permutation(T)[:I]
    idx2 = np.random.permutation(M)[:I]
    fd = mx_kscale(D)
    fq = mx_kscale(Q)
    keysp = pack_weight(n((D, T)) / fd[:, None], "e4m3")
    return {
        "query": (n((D, Q)) * 1.0 / np.sqrt(D) * fd[:, None]).astype(np.float32),
        "query2": (n((D, Q)) * 1.0 / np.sqrt(D) * fd[:, None]).astype(np.float32),
        "query3": (n((D, Q)) * 0.8 / np.sqrt(D) * fd[:, None]).astype(np.float32),
        "keys_words": keysp[0],
        "keys_scales": keysp[1],
        "eager": (np.random.uniform(0.8, 2.0, (Q, 1))).astype(np.float32),
        "thresh": (np.random.uniform(1.5, 4.0, (Q, 1))).astype(np.float32),
        "qs": (np.random.uniform(20.0, 80.0, (Q, 1)) * fq[:, None]).astype(np.float32),
        "msgs": (n((Q, E)) * 1 / np.sqrt(Q) / fq[:, None]).astype(np.float32),
        "old": (n((E, M)) * 1.0).astype(np.float32),
        "fade": (np.random.uniform(0.3, 0.9, (1, M))).astype(np.float32),
        "offs": striped(idx),
        "offs2": striped(idx2),
    }


def reference(query, query2, query3, keys_words, keys_scales, eager, thresh, qs, msgs, old, fade, offs, offs2):
    idx = unstriped(offs)
    idx2 = unstriped(offs2)
    keysu = unpack_weight(keys_words, keys_scales, "e4m3")
    queryq = mxq(f64(query), 0, "e4m3")
    keysidxg = keysu[:, idx]
    a = queryq.T @ keysidxg
    query2q = mxq(f64(query2), 0, "e4m3")
    b = query2q.T @ keysidxg
    query3q = mxq(f64(query3), 0, "e4m3")
    b3 = query3q.T @ keysidxg
    s = a * sigmoid(b - b3) + b3
    m0 = np.max(s, axis=1, keepdims=True)
    m1 = np.mean(s, axis=1, keepdims=True)
    p = np.exp(s - m0)
    gt0 = sigmoid((m0 - m1) * f64(eager) - f64(thresh))
    w = p / np.sum(p, axis=1, keepdims=True) * gt0
    wq = w * f64(qs)
    msgsq = mxq(f64(msgs), 0, "e4m3")
    wqq = mxq(wq, 0, "e4m3")
    dl = msgsq.T @ wqq
    df = np.zeros((E, M))
    df[:, idx2] = dl
    y = f64(old) * f64(fade) + df
    return y

@@ -1,0 +1,279 @@
+from contextlib import ExitStack
+
+import concourse.mybir as mybir
+from concourse.masks import make_identity
+
+F32 = mybir.dt.float32
+BF16 = mybir.dt.bfloat16
+I32 = mybir.dt.int32
+U32 = mybir.dt.uint32
+U16 = mybir.dt.uint16
+U8 = mybir.dt.uint8
+FP8X4 = mybir.dt.float8_e4m3fn_x4
+ALU = mybir.AluOpType
+ACT = mybir.ActivationFunctionType
+AX = mybir.AxisListType
+
+P = 128
+PACK = 4
+D, T, I, Q, E, M = 512, 2048, 512, 512, 512, 1024
+FLOPS = 4 * 2 * 512 * 512 * 512
+
+
+def tile_attend_threeviews_abstaining_delivered_kernel(
+    tc, query, query2, query3, keys_words, keys_scales, eager, thresh, qs, msgs, old, fade, offs, offs2, out
+):
+    nc = tc.nc
+    with ExitStack() as ctx:
+        lists = ctx.enter_context(tc.tile_pool(name="lists", bufs=1))
+        sb = ctx.enter_context(tc.tile_pool(name="sb", bufs=1))
+        ps = ctx.enter_context(tc.psum_pool(name="ps", bufs=1))
+
+        def tile(name, shape, dtype, tag=None):
+            return sb.tile(shape, dtype, name=name, tag=tag or name, align_bytes=64)
+
+        def bank(n, name):
+            return ps.tile([P, 512], F32, name=name, tag="bank%d" % n)
+
+        key_bytes = tile("key_bytes", [P, T], U8)
+        nc.vector.memset(key_bytes[:].bitcast(I32), 0)
+        key_list = lists.tile([P, I // 16], U16, name="key_list")
+        nc.sync.dma_start(key_list[:], offs)
+        fade_cols = tile("fade_cols", [P, 8], F32)
+        nc.sync.dma_start(fade_cols[:], fade.rearrange("o (p c) -> p (o c)", c=8))
+        key_words = tile("key_words", [P, T], U32)
+        nc.sync.dma_start(key_words[:].bitcast(I32), keys_words[0].rearrange("p n t -> p (n t)").bitcast(I32))
+        for g in range(4):
+            nc.sync.dma_start(
+                key_bytes[32 * g : 32 * g + 4, :].bitcast(I32), keys_scales[0, 4 * g : 4 * g + 4, :].bitcast(I32)
+            )
+        raw = {}
+        for name, src in (("b", query2), ("c", query3), ("a", query)):
+            raw[name] = tile("raw_" + name, [P, PACK, Q], F32)
+            nc.sync.dma_start(raw[name][:], src.rearrange("(p j) q -> p j q", j=PACK))
+        rowvec = {}
+        for name, src in (("eager", eager), ("thresh", thresh), ("qs", qs)):
+            rowvec[name] = tile("v_" + name, [P, PACK], F32)
+            nc.sync.dma_start(rowvec[name][:], src.rearrange("(p r) o -> p (r o)", r=PACK))
+        old_sb = [tile("old%d" % e, [P, M], F32) for e in range(4)]
+        raw_m = tile("raw_m", [P, PACK, E], F32)
+        nc.sync.dma_start(raw_m[:], msgs.rearrange("(p r) e -> p r e", r=PACK))
+        for e in range(4):
+            nc.sync.dma_start(old_sb[e][:], old[e * P : (e + 1) * P, :])
+        col_list = lists.tile([P, I // 16], U16, name="col_list")
+        nc.sync.dma_start(col_list[:], offs2)
+
+        window = [tile("window%d" % e, [P, M], F32) for e in range(4)]
+        for e in range(4):
+            nc.vector.memset(window[e][:], 0.0)
+        ident = tile("ident", [P, P], F32)
+        make_identity(nc, ident[:])
+        fade_row = tile("fade_row", [P, P, 8], F32)
+        for h in range(2):
+            spread = bank(6 + h, "spread%d" % h)
+            for c in range(4):
+                col = 4 * h + c
+                nc.tensor.transpose(
+                    spread[:, c * P : (c + 1) * P], fade_cols[:, col : col + 1].to_broadcast([P, P]), ident[:]
+                )
+            nc.scalar.copy(fade_row[:, :, 4 * h : 4 * h + 4], spread[:].rearrange("p (c n) -> p n c", c=4))
+
+        kb = tile("kb", [P, I], U8)
+        nc.vector.tensor_copy(kb[:], key_bytes[:].indirect(key_list[:]))
+        kw = tile("kw", [P, I], U32)
+        nc.vector.tensor_copy(kw[:], key_words[:].indirect(key_list[:]))
+
+        def lay_pair(name, h, sign):
+            laid = tile("laid_%s%d" % (name, h), [P, 2, P, PACK], BF16)
+            dst = laid[:].rearrange("p t m j -> p m t j")
+            src = raw[name][:].rearrange("p j (m t) -> p m t j", t=PACK)[:, :, 2 * h : 2 * h + 2, :]
+            if h == 0:
+                nc.vector.tensor_scalar(dst, src, sign, None, ALU.mult)
+            else:
+                nc.scalar.activation(dst, src, ACT.Copy, scale=sign)
+            return laid[:].rearrange("p t m j -> p (t m j)")
+
+        def quantise(name, laid, width):
+            words = tile("w_" + name, [P, width], U32)
+            scales = tile("s_" + name, [P, width], U8)
+            nc.vector.quantize_mx(words[:].bitcast(FP8X4), scales[:], laid)
+            return words, scales
+
+        def score(dst, operand, r, start, stop):
+            words, scales = operand[r // 2]
+            cols = slice((r % 2) * P, (r % 2 + 1) * P)
+            nc.tensor.matmul_mx(
+                dst[:], lhsT=words[:, cols].bitcast(FP8X4), lhsT_scale=scales[:, cols],
+                rhs=kw[:].bitcast(FP8X4), rhs_scale=kb[:], start=start, stop=stop,
+            )
+
+        diff = [bank(r, "diff%d" % r) for r in range(4)]
+        laid_b = [lay_pair("b", h, 1.0) for h in range(2)]
+        qb = []
+        for h in range(2):
+            qb.append(quantise("b%d" % h, laid_b[h], 2 * P))
+            for r in (2 * h, 2 * h + 1):
+                score(diff[r], qb, r, True, False)
+        laid_c = [lay_pair("c", h, -1.0) for h in range(2)]
+        qc = []
+        neg_b3 = [bank(4 + r, "negb3_%d" % r) for r in range(4)]
+        th = [tile("th%d" % r, [P, I], F32) for r in range(4)]
+        for h in range(2):
+            qc.append(quantise("c%d" % h, laid_c[h], 2 * P))
+            for r in (2 * h, 2 * h + 1):
+                score(diff[r], qc, r, False, True)
+        for r in range(2):
+            nc.scalar.activation(th[r][:], diff[r][:], ACT.Tanh, scale=0.5)
+        for r in range(4):
+            score(neg_b3[r], qc, r, True, True)
+        laid_a = [lay_pair("a", h, 1.0) for h in range(2)]
+        for r in range(2, 4):
+            nc.scalar.activation(th[r][:], diff[r][:], ACT.Tanh, scale=0.5)
+        qa = []
+        a_ps = []
+        for h in range(2):
+            qa.append(quantise("a%d" % h, laid_a[h], 2 * P))
+            for r in (2 * h, 2 * h + 1):
+                a_ps.append(bank(r, "a%d" % r))
+                score(a_ps[r], qa, r, True, True)
+
+        def scaled(name, src, factor):
+            t = tile(name, [P, PACK], F32)
+            nc.gpsimd.tensor_scalar(t[:], src[:], factor, 0.0, ALU.mult, ALU.add)
+            return t
+
+        mean_gain = scaled("mean_gain", rowvec["eager"], 0.5 / I)
+        max_gain = scaled("max_gain", rowvec["eager"], -0.5)
+        neg_half_thresh = scaled("neg_half_thresh", rowvec["thresh"], -0.5)
+        half_qs = scaled("half_qs", rowvec["qs"], 0.5)
+
+        u = [tile("u%d" % r, [P, I], F32) for r in range(4)]
+        neg_s = [tile("neg_s%d" % r, [P, I], F32) for r in range(4)]
+        p = [tile("p%d" % r, [P, I], F32) for r in range(4)]
+        wq = tile("wq", [P, PACK, I], BF16)
+
+        def stat(name):
+            return [tile("%s%d" % (name, r), [P, 1], F32) for r in range(4)]
+
+        neg_sum, neg_max, p_sum, inv_sum = stat("neg_sum"), stat("neg_max"), stat("p_sum"), stat("inv_sum")
+        gate_bias, gate_tanh, gate_qs, factor = stat("gate_bias"), stat("gate_tanh"), stat("gate_qs"), stat("factor")
+
+        def gated(r):
+            nc.vector.scalar_tensor_tensor(u[r][:], th[r][:], 1.0, a_ps[r][:], ALU.add, ALU.mult)
+
+        def summed(r):
+            nc.vector.scalar_tensor_tensor(
+                neg_s[r][:], u[r][:], -0.5, neg_b3[r][:], ALU.mult, ALU.add, accum_out=neg_sum[r][:]
+            )
+            nc.scalar.activation(
+                gate_bias[r][:], neg_sum[r][:], ACT.Identity,
+                scale=mean_gain[:, r : r + 1], bias=neg_half_thresh[:, r : r + 1],
+            )
+
+        def weigh(r):
+            nc.vector.tensor_reduce(neg_max[r][:], neg_s[r][:], AX.X, ALU.min)
+            nc.scalar.activation(
+                gate_tanh[r][:], neg_max[r][:], ACT.Tanh, scale=max_gain[:, r : r + 1], bias=gate_bias[r][:]
+            )
+            nc.scalar.activation(
+                p[r][:], neg_s[r][:], ACT.Exp, scale=-1.0, bias=neg_max[r][:], accum_out=p_sum[r][:]
+            )
+            nc.scalar.activation(
+                gate_qs[r][:], gate_tanh[r][:], ACT.Identity,
+                scale=half_qs[:, r : r + 1], bias=half_qs[:, r : r + 1],
+            )
+
+        def finish(r, first):
+            nc.vector.reciprocal(inv_sum[r][:], p_sum[r][:])
+            if first:
+                nc.vector.tensor_scalar(
+                    wq[:, r, :first], p[r][:, :first], inv_sum[r][:], gate_qs[r][:], ALU.mult, ALU.mult
+                )
+            nc.scalar.activation(factor[r][:], inv_sum[r][:], ACT.Copy, scale=gate_qs[r][:])
+            nc.scalar.activation(wq[:, r, first:], p[r][:, first:], ACT.Copy, scale=factor[r][:])
+
+        fade_flat = fade_row[:].rearrange("p n c -> p (n c)")
+
+        def faded(dst, e):
+            for h in range(2):
+                cols = slice(h * 512, (h + 1) * 512)
+                nc.gpsimd.tensor_tensor(dst[:, cols], old_sb[e][:, cols], fade_flat[:, cols], ALU.mult)
+
+        laid_m = [tile("laid_m%d" % h, [P, 2 * P, PACK], BF16) for h in range(2)]
+        m_src = raw_m[:].rearrange("p r e -> p e r")
+        nc.gpsimd.tensor_scalar(laid_m[0][:], m_src[:, : 2 * P, :], 1.0, 0.0, ALU.mult, ALU.add)
+        gated(0)
+        gated(1)
+        summed(0)
+        gated(2)
+        weigh(0)
+        summed(1)
+        gated(3)
+        weigh(1)
+        finish(0, 0)
+        nc.scalar.copy(laid_m[1][:], m_src[:, 2 * P :, :])
+        summed(2)
+        weigh(2)
+        finish(1, 0)
+        summed(3)
+        qm = [quantise("m0", laid_m[0][:].rearrange("p e r -> p (e r)"), 2 * P)]
+        weigh(3)
+        finish(2, 0)
+        qm.append(quantise("m1", laid_m[1][:].rearrange("p e r -> p (e r)"), 2 * P))
+        finish(3, 2 * P)
+        kept = [old_sb[0], old_sb[1]]
+        faded(old_sb[0], 0)
+        faded(old_sb[1], 1)
+
+        w_src = wq[:].rearrange("p r i -> p i r")
+        pieces = ((0, P), (P, 2 * P), (2 * P, I))
+        laid_w = [tile("laid_w%d" % n, [P, hi - lo, PACK], BF16) for n, (lo, hi) in enumerate(pieces)]
+        nc.vector.tensor_copy(laid_w[0][:], w_src[:, 0:P, :])
+        nc.vector.tensor_copy(laid_w[1][:], w_src[:, P : 2 * P, :])
+        nc.scalar.copy(laid_w[2][:], w_src[:, 2 * P :, :])
+        w_words = tile("w_words", [P, I], U32)
+        w_scales = tile("w_scales", [P, I], U8)
+        dl = [tile("dl%d" % e, [P, I], F32) for e in range(4)]
+
+        def deliver(dst, e, lo, hi):
+            words, scales = qm[e // 2]
+            cols = slice((e % 2) * P, (e % 2 + 1) * P)
+            nc.tensor.matmul_mx(
+                dst[:, lo:hi], lhsT=words[:, cols].bitcast(FP8X4), lhsT_scale=scales[:, cols],
+                rhs=w_words[:, lo:hi].bitcast(FP8X4), rhs_scale=w_scales[:, lo:hi], start=True, stop=True,
+            )
+
+        def scatter(e, lo, hi):
+            nc.vector.tensor_copy(window[e][:].indirect(col_list[:, lo // 16 : hi // 16]), dl[e][:, lo:hi])
+
+        first_bank = bank(4, "dl_first")
+        rest_bank = bank(5, "dl_rest")
+        for n, (lo, hi) in enumerate(pieces):
+            nc.vector.quantize_mx(
+                w_words[:, lo:hi].bitcast(FP8X4), w_scales[:, lo:hi], laid_w[n][:].rearrange("p i r -> p (i r)")
+            )
+            deliver(first_bank if n == 0 else rest_bank, 0, lo, hi)
+            if n == 0:
+                nc.scalar.copy(dl[0][:, :P], first_bank[:, :P])
+        nc.scalar.copy(dl[0][:, P:], rest_bank[:, P:])
+        for e, n in ((1, 6), (2, 0), (3, 1)):
+            whole = bank(n, "dl_whole%d" % e)
+            deliver(whole, e, 0, I)
+            nc.scalar.copy(dl[e][:], whole[:])
+
+        late = tile("late", [P, 2, M], F32, tag="laid_w2")
+        for e in (2, 3):
+            kept.append(late[:, e - 2, :])
+            faded(kept[e], e)
+
+        scatter(0, 0, P)
+        scatter(0, P, I)
+        for e in range(4):
+            if e:
+                scatter(e, 0, I)
+            for h in range(2):
+                cols = slice(h * 512, (h + 1) * 512)
+                engine = nc.vector if e == 3 else nc.gpsimd
+                engine.tensor_tensor(kept[e][:, cols], kept[e][:, cols], window[e][:, cols], ALU.add)
+                queue = nc.scalar if (e == 3 and h == 1) else nc.sync
+                queue.dma_start(out[e * P : (e + 1) * P, cols], kept[e][:, cols])

@@ -70,13 +70,22 @@ def tile_attend_threeviews_abstaining_delivered_kernel(
         make_identity(nc, ident[:])
         fade_row = tile("fade_row", [P, P, 8], F32)
         for h in range(2):
-            spread = bank(6 + h, "spread%d" % h)
+            spread = bank(2 + h, "spread%d" % h)
             for c in range(4):
                 col = 4 * h + c
                 nc.tensor.transpose(
                     spread[:, c * P : (c + 1) * P], fade_cols[:, col : col + 1].to_broadcast([P, P]), ident[:]
                 )
             nc.scalar.copy(fade_row[:, :, 4 * h : 4 * h + 4], spread[:].rearrange("p (c n) -> p n c", c=4))
+
+        fade_flat = fade_row[:].rearrange("p n c -> p (n c)")
+        fade_part = tile("fade_part", [P, 8], F32)
+        for h in range(2):
+            turned = bank(h, "fade_turned%d" % h)
+            for c in range(4):
+                col = 4 * h + c
+                nc.tensor.transpose(turned[:, c * P : (c + 1) * P], fade_flat[:, col * P : (col + 1) * P], ident[:])
+            nc.scalar.copy(fade_part[:, 4 * h : 4 * h + 4], turned[:, 0:512:P])
 
         kb = tile("kb", [P, I], U8)
         nc.vector.tensor_copy(kb[:], key_bytes[:].indirect(key_list[:]))
@@ -87,14 +96,16 @@ def tile_attend_threeviews_abstaining_delivered_kernel(
             laid = tile("laid_%s%d" % (name, h), [P, 2, P, PACK], BF16)
             dst = laid[:].rearrange("p t m j -> p m t j")
             src = raw[name][:].rearrange("p j (m t) -> p m t j", t=PACK)[:, :, 2 * h : 2 * h + 2, :]
-            if h == 0:
+            if h == 0 and sign == 1.0:
+                nc.vector.tensor_copy(dst, src)
+            elif h == 0:
                 nc.vector.tensor_scalar(dst, src, sign, None, ALU.mult)
             else:
                 nc.scalar.activation(dst, src, ACT.Copy, scale=sign)
             return laid[:].rearrange("p t m j -> p (t m j)")
 
-        def quantise(name, laid, width):
-            words = tile("w_" + name, [P, width], U32)
+        def quantise(name, laid, width, tag=None):
+            words = tile("w_" + name, [P, width], U32, tag=tag)
             scales = tile("s_" + name, [P, width], U8)
             nc.vector.quantize_mx(words[:].bitcast(FP8X4), scales[:], laid)
             return words, scales
@@ -116,7 +127,6 @@ def tile_attend_threeviews_abstaining_delivered_kernel(
                 score(diff[r], qb, r, True, False)
         laid_c = [lay_pair("c", h, -1.0) for h in range(2)]
         qc = []
-        neg_b3 = [bank(4 + r, "negb3_%d" % r) for r in range(4)]
         th = [tile("th%d" % r, [P, I], F32) for r in range(4)]
         for h in range(2):
             qc.append(quantise("c%d" % h, laid_c[h], 2 * P))
@@ -124,18 +134,32 @@ def tile_attend_threeviews_abstaining_delivered_kernel(
                 score(diff[r], qc, r, False, True)
         for r in range(2):
             nc.scalar.activation(th[r][:], diff[r][:], ACT.Tanh, scale=0.5)
-        for r in range(4):
-            score(neg_b3[r], qc, r, True, True)
         laid_a = [lay_pair("a", h, 1.0) for h in range(2)]
         for r in range(2, 4):
             nc.scalar.activation(th[r][:], diff[r][:], ACT.Tanh, scale=0.5)
         qa = []
         a_ps = []
-        for h in range(2):
-            qa.append(quantise("a%d" % h, laid_a[h], 2 * P))
-            for r in (2 * h, 2 * h + 1):
-                a_ps.append(bank(r, "a%d" % r))
-                score(a_ps[r], qa, r, True, True)
+        a_words = tile("w_a0", [P, 2 * P], U32)
+        a_scales = tile("s_a0", [P, 2 * P], U8)
+        qa.append((a_words, a_scales))
+        neg_b3 = []
+
+        def score_a(r, n):
+            a_ps.append(bank(n, "a%d" % r))
+            score(a_ps[r], qa, r, True, True)
+
+        def score_b3(r, n):
+            neg_b3.append(bank(n, "negb3_%d" % r))
+            score(neg_b3[r], qc, r, True, True)
+
+        for r in range(2):
+            cols = slice(r * P, (r + 1) * P)
+            nc.vector.quantize_mx(
+                a_words[:, cols].bitcast(FP8X4), a_scales[:, cols], laid_a[0][:, r * 512 : (r + 1) * 512]
+            )
+            score_a(r, 6 + r)
+        score_b3(0, 0)
+        score_b3(1, 1)
 
         def scaled(name, src, factor):
             t = tile(name, [P, PACK], F32)
@@ -156,7 +180,7 @@ def tile_attend_threeviews_abstaining_delivered_kernel(
             return [tile("%s%d" % (name, r), [P, 1], F32) for r in range(4)]
 
         neg_sum, neg_max, p_sum, inv_sum = stat("neg_sum"), stat("neg_max"), stat("p_sum"), stat("inv_sum")
-        gate_bias, gate_tanh, gate_qs, factor = stat("gate_bias"), stat("gate_tanh"), stat("gate_qs"), stat("factor")
+        gate_bias, gate_tanh, gate_qs, factor = stat("gate_bias"), stat("gate_tanh"), stat("gate_qs"), {r: tile("factor%d" % r, [P, 1], F32) for r in (3,)}
 
         def gated(r):
             nc.vector.scalar_tensor_tensor(u[r][:], th[r][:], 1.0, a_ps[r][:], ALU.add, ALU.mult)
@@ -185,6 +209,9 @@ def tile_attend_threeviews_abstaining_delivered_kernel(
 
         def finish(r, first):
             nc.vector.reciprocal(inv_sum[r][:], p_sum[r][:])
+            if r < 3:
+                nc.gpsimd.tensor_scalar(wq[:, r, :], p[r][:], inv_sum[r][:], gate_qs[r][:], ALU.mult, ALU.mult)
+                return
             if first:
                 nc.vector.tensor_scalar(
                     wq[:, r, :first], p[r][:, :first], inv_sum[r][:], gate_qs[r][:], ALU.mult, ALU.mult
@@ -192,18 +219,21 @@ def tile_attend_threeviews_abstaining_delivered_kernel(
             nc.scalar.activation(factor[r][:], inv_sum[r][:], ACT.Copy, scale=gate_qs[r][:])
             nc.scalar.activation(wq[:, r, first:], p[r][:, first:], ACT.Copy, scale=factor[r][:])
 
-        fade_flat = fade_row[:].rearrange("p n c -> p (n c)")
-
         def faded(dst, e):
             for h in range(2):
                 cols = slice(h * 512, (h + 1) * 512)
                 nc.gpsimd.tensor_tensor(dst[:, cols], old_sb[e][:, cols], fade_flat[:, cols], ALU.mult)
 
-        laid_m = [tile("laid_m%d" % h, [P, 2 * P, PACK], BF16) for h in range(2)]
         m_src = raw_m[:].rearrange("p r e -> p e r")
-        nc.gpsimd.tensor_scalar(laid_m[0][:], m_src[:, : 2 * P, :], 1.0, 0.0, ALU.mult, ALU.add)
         gated(0)
+        qa.append(quantise("a1", laid_a[1], 2 * P, tag="th0"))
+        score_a(2, 2)
+        score_a(3, 3)
+        score_b3(2, 6)
+        laid_m = [tile("laid_m0", [P, 2 * P, PACK], BF16, tag="laid_a1"), tile("laid_m1", [P, 2 * P, PACK], BF16)]
+        nc.gpsimd.tensor_scalar(laid_m[0][:], m_src[:, : 2 * P, :], 1.0, 0.0, ALU.mult, ALU.add)
         gated(1)
+        score_b3(3, 7)
         summed(0)
         gated(2)
         weigh(0)
@@ -217,13 +247,10 @@ def tile_attend_threeviews_abstaining_delivered_kernel(
         finish(1, 0)
         summed(3)
         qm = [quantise("m0", laid_m[0][:].rearrange("p e r -> p (e r)"), 2 * P)]
-        weigh(3)
         finish(2, 0)
+        weigh(3)
         qm.append(quantise("m1", laid_m[1][:].rearrange("p e r -> p (e r)"), 2 * P))
         finish(3, 2 * P)
-        kept = [old_sb[0], old_sb[1]]
-        faded(old_sb[0], 0)
-        faded(old_sb[1], 1)
 
         w_src = wq[:].rearrange("p r i -> p i r")
         pieces = ((0, P), (P, 2 * P), (2 * P, I))
@@ -246,34 +273,73 @@ def tile_attend_threeviews_abstaining_delivered_kernel(
         def scatter(e, lo, hi):
             nc.vector.tensor_copy(window[e][:].indirect(col_list[:, lo // 16 : hi // 16]), dl[e][:, lo:hi])
 
-        first_bank = bank(4, "dl_first")
-        rest_bank = bank(5, "dl_rest")
         for n, (lo, hi) in enumerate(pieces):
             nc.vector.quantize_mx(
                 w_words[:, lo:hi].bitcast(FP8X4), w_scales[:, lo:hi], laid_w[n][:].rearrange("p i r -> p (i r)")
             )
-            deliver(first_bank if n == 0 else rest_bank, 0, lo, hi)
-            if n == 0:
-                nc.scalar.copy(dl[0][:, :P], first_bank[:, :P])
-        nc.scalar.copy(dl[0][:, P:], rest_bank[:, P:])
-        for e, n in ((1, 6), (2, 0), (3, 1)):
+            part = bank((4, 5, 6)[n], "dl_part%d" % n)
+            deliver(part, 0, lo, hi)
+            nc.scalar.copy(dl[0][:, lo:hi], part[:, lo:hi])
+        for e, n in ((1, 0), (2, 1), (3, 2)):
             whole = bank(n, "dl_whole%d" % e)
             deliver(whole, e, 0, I)
             nc.scalar.copy(dl[e][:], whole[:])
 
         late = tile("late", [P, 2, M], F32, tag="laid_w2")
-        for e in (2, 3):
-            kept.append(late[:, e - 2, :])
-            faded(kept[e], e)
+        for e in (1, 2):
+            faded(late[:, e - 1, :], e)
 
-        scatter(0, 0, P)
-        scatter(0, P, I)
-        for e in range(4):
-            if e:
-                scatter(e, 0, I)
+        kept_t = tile("kept_t", [P, 8, 2 * P], F32, tag="laid_w1")
+        for n, b in enumerate((3, 7, 4, 5)):
+            turned = bank(b, "old_turned%d" % n)
+            for k in range(2):
+                c = 2 * n + k
+                for slot, e in enumerate((0, 3)):
+                    lo = (2 * k + slot) * P
+                    nc.tensor.transpose(turned[:, lo : lo + P], old_sb[e][:, c * P : (c + 1) * P], ident[:])
+            for k in range(2):
+                c = 2 * n + k
+                nc.scalar.activation(
+                    kept_t[:, c, :], turned[:, 2 * k * P : 2 * (k + 1) * P], ACT.Copy, scale=fade_part[:, c : c + 1]
+                )
+
+        def store(e, h, src, queue):
+            queue.dma_start(out[e * P : (e + 1) * P, h * 512 : (h + 1) * 512], src)
+
+        for lo, hi in pieces:
+            scatter(0, lo, hi)
+        window_t = tile("window_t", [P, 8, P], F32)
+        result0 = tile("result0", [P, M], F32)
+        for h in range(2):
+            turned = bank((6, 0)[h], "window_turned%d" % h)
+            for k in range(4):
+                c = 4 * h + k
+                nc.tensor.transpose(turned[:, k * P : (k + 1) * P], window[0][:, c * P : (c + 1) * P], ident[:])
+            nc.scalar.copy(window_t[:, 4 * h : 4 * h + 4, :], turned[:].rearrange("p (k e) -> p k e", k=4))
+        for h in range(2):
+            summed_back = bank(1 + h, "result_back%d" % h)
+            for k in range(4):
+                c = 4 * h + k
+                dst = summed_back[:, k * P : (k + 1) * P]
+                nc.tensor.matmul(dst, kept_t[:, c, :P], ident[:], start=True, stop=False, is_transpose=True)
+                nc.tensor.matmul(dst, window_t[:, c, :], ident[:], start=False, stop=True, is_transpose=True)
+            nc.scalar.copy(result0[:, h * 512 : (h + 1) * 512], summed_back[:])
+            store(0, h, result0[:, h * 512 : (h + 1) * 512], nc.scalar)
+        kept3 = []
+        for h in range(2):
+            back = bank((3, 7)[h], "kept_back%d" % h)
+            for k in range(4):
+                nc.tensor.transpose(back[:, k * P : (k + 1) * P], kept_t[:, 4 * h + k, P:], ident[:])
+            kept3.append(back)
+        for e in (1, 2):
+            scatter(e, 0, I)
             for h in range(2):
                 cols = slice(h * 512, (h + 1) * 512)
-                engine = nc.vector if e == 3 else nc.gpsimd
-                engine.tensor_tensor(kept[e][:, cols], kept[e][:, cols], window[e][:, cols], ALU.add)
-                queue = nc.scalar if (e == 3 and h == 1) else nc.sync
-                queue.dma_start(out[e * P : (e + 1) * P, cols], kept[e][:, cols])
+                nc.gpsimd.tensor_tensor(late[:, e - 1, cols], late[:, e - 1, cols], window[e][:, cols], ALU.add)
+                store(e, h, late[:, e - 1, cols], nc.sync)
+        scatter(3, 0, I)
+        result3 = tile("result3", [P, M], F32)
+        for h in range(2):
+            cols = slice(h * 512, (h + 1) * 512)
+            nc.vector.tensor_tensor(result3[:, cols], window[3][:, cols], kept3[h][:], ALU.add)
+            store(3, h, result3[:, cols], nc.sync)

@@ -37,12 +37,16 @@ def tile_attend_threeviews_abstaining_delivered_kernel(
 
         key_bytes = tile("key_bytes", [P, T], U8)
         nc.vector.memset(key_bytes[:].bitcast(I32), 0)
-        key_list = lists.tile([P, I // 16], U16, name="key_list")
-        nc.sync.dma_start(key_list[:], offs)
+        warm = tile("warm", [P, 1], F32)
+        nc.gpsimd.memset(warm[:], 0.0)
         fade_cols = tile("fade_cols", [P, 8], F32)
         nc.sync.dma_start(fade_cols[:], fade.rearrange("o (p c) -> p (o c)", c=8))
         key_words = tile("key_words", [P, T], U32)
         nc.sync.dma_start(key_words[:].bitcast(I32), keys_words[0].rearrange("p n t -> p (n t)").bitcast(I32))
+        key_list = lists.tile([P, I // 16], U16, name="key_list")
+        nc.sync.dma_start(key_list[:], offs)
+        warmed = tile("warmed", [P, 1], F32)
+        nc.scalar.activation(warmed[:], warm[:], ACT.Exp)
         for g in range(4):
             nc.sync.dma_start(
                 key_bytes[32 * g : 32 * g + 4, :].bitcast(I32), keys_scales[0, 4 * g : 4 * g + 4, :].bitcast(I32)
@@ -87,10 +91,10 @@ def tile_attend_threeviews_abstaining_delivered_kernel(
                 nc.tensor.transpose(turned[:, c * P : (c + 1) * P], fade_flat[:, col * P : (col + 1) * P], ident[:])
             nc.scalar.copy(fade_part[:, 4 * h : 4 * h + 4], turned[:, 0:512:P])
 
-        kb = tile("kb", [P, I], U8)
-        nc.vector.tensor_copy(kb[:], key_bytes[:].indirect(key_list[:]))
         kw = tile("kw", [P, I], U32)
         nc.vector.tensor_copy(kw[:], key_words[:].indirect(key_list[:]))
+        kb = tile("kb", [P, I], U8)
+        nc.vector.tensor_copy(kb[:], key_bytes[:].indirect(key_list[:]))
 
         def lay_pair(name, h, sign):
             laid = tile("laid_%s%d" % (name, h), [P, 2, P, PACK], BF16)
@@ -213,9 +217,10 @@ def tile_attend_threeviews_abstaining_delivered_kernel(
                 nc.gpsimd.tensor_scalar(wq[:, r, :], p[r][:], inv_sum[r][:], gate_qs[r][:], ALU.mult, ALU.mult)
                 return
             if first:
-                nc.vector.tensor_scalar(
-                    wq[:, r, :first], p[r][:, :first], inv_sum[r][:], gate_qs[r][:], ALU.mult, ALU.mult
-                )
+                for lo in range(0, first, P):
+                    nc.vector.tensor_scalar(
+                        wq[:, r, lo : lo + P], p[r][:, lo : lo + P], inv_sum[r][:], gate_qs[r][:], ALU.mult, ALU.mult
+                    )
             nc.scalar.activation(factor[r][:], inv_sum[r][:], ACT.Copy, scale=gate_qs[r][:])
             nc.scalar.activation(wq[:, r, first:], p[r][:, first:], ACT.Copy, scale=factor[r][:])
 
@@ -243,13 +248,15 @@ def tile_attend_threeviews_abstaining_delivered_kernel(
         finish(0, 0)
         nc.scalar.copy(laid_m[1][:], m_src[:, 2 * P :, :])
         summed(2)
+        summed(3)
         weigh(2)
         finish(1, 0)
-        summed(3)
-        qm = [quantise("m0", laid_m[0][:].rearrange("p e r -> p (e r)"), 2 * P)]
-        finish(2, 0)
         weigh(3)
-        qm.append(quantise("m1", laid_m[1][:].rearrange("p e r -> p (e r)"), 2 * P))
+        finish(2, 0)
+        qm = [
+            quantise("m%d" % h, laid_m[h][:].rearrange("p e r -> p (e r)"), 2 * P, tag=("u3", "neg_s2")[h])
+            for h in range(2)
+        ]
         finish(3, 2 * P)
 
         w_src = wq[:].rearrange("p r i -> p i r")
@@ -338,8 +345,10 @@ def tile_attend_threeviews_abstaining_delivered_kernel(
                 nc.gpsimd.tensor_tensor(late[:, e - 1, cols], late[:, e - 1, cols], window[e][:, cols], ALU.add)
                 store(e, h, late[:, e - 1, cols], nc.sync)
         scatter(3, 0, I)
-        result3 = tile("result3", [P, M], F32)
-        for h in range(2):
-            cols = slice(h * 512, (h + 1) * 512)
-            nc.vector.tensor_tensor(result3[:, cols], window[3][:, cols], kept3[h][:], ALU.add)
-            store(3, h, result3[:, cols], nc.sync)
+        result3 = tile("result3", [P, M], F32, tag="result0")
+        for lo, hi, queue in ((0, 512, nc.sync), (512, 768, nc.scalar), (768, M, nc.sync)):
+            h = lo // 512
+            nc.vector.tensor_tensor(
+                result3[:, lo:hi], window[3][:, lo:hi], kept3[h][:, lo - 512 * h : hi - 512 * h], ALU.add
+            )
+            queue.dma_start(out[3 * P :, lo:hi], result3[:, lo:hi])

@@ -165,15 +165,11 @@ def tile_attend_threeviews_abstaining_delivered_kernel(
         score_b3(0, 0)
         score_b3(1, 1)
 
-        def scaled(name, src, factor):
-            t = tile(name, [P, PACK], F32)
-            nc.gpsimd.tensor_scalar(t[:], src[:], factor, 0.0, ALU.mult, ALU.add)
-            return t
-
-        mean_gain = scaled("mean_gain", rowvec["eager"], 0.5 / I)
-        max_gain = scaled("max_gain", rowvec["eager"], -0.5)
-        neg_half_thresh = scaled("neg_half_thresh", rowvec["thresh"], -0.5)
-        half_qs = scaled("half_qs", rowvec["qs"], 0.5)
+        row_consts = tile("row_consts", [P, 4, PACK], F32, tag="laid_a0")
+        terms = (("eager", 0.5 / I), ("thresh", -0.5), ("eager", -0.5), ("qs", 0.5))
+        for n, (name, times) in enumerate(terms):
+            nc.gpsimd.tensor_scalar(row_consts[:, n, :], rowvec[name][:], times, 0.0, ALU.mult, ALU.add)
+        mean_gain, neg_half_thresh, max_gain, half_qs = [row_consts[:, n, :] for n in range(4)]
 
         u = [tile("u%d" % r, [P, I], F32) for r in range(4)]
         neg_s = [tile("neg_s%d" % r, [P, I], F32) for r in range(4)]
@@ -214,7 +210,7 @@ def tile_attend_threeviews_abstaining_delivered_kernel(
         def finish(r, first):
             nc.vector.reciprocal(inv_sum[r][:], p_sum[r][:])
             if r < 3:
-                nc.gpsimd.tensor_scalar(wq[:, r, :], p[r][:], inv_sum[r][:], gate_qs[r][:], ALU.mult, ALU.mult)
+                (nc.vector if r == 2 else nc.gpsimd).tensor_scalar(wq[:, r, :], p[r][:], inv_sum[r][:], gate_qs[r][:], ALU.mult, ALU.mult)
                 return
             if first:
                 for lo in range(0, first, P):
@@ -249,12 +245,12 @@ def tile_attend_threeviews_abstaining_delivered_kernel(
         nc.scalar.copy(laid_m[1][:], m_src[:, 2 * P :, :])
         summed(2)
         summed(3)
-        weigh(2)
         finish(1, 0)
+        weigh(2)
         weigh(3)
         finish(2, 0)
         qm = [
-            quantise("m%d" % h, laid_m[h][:].rearrange("p e r -> p (e r)"), 2 * P, tag=("u3", "neg_s2")[h])
+            quantise("m%d" % h, laid_m[h][:].rearrange("p e r -> p (e r)"), 2 * P, tag=("neg_s1", "neg_s2")[h])
             for h in range(2)
         ]
         finish(3, 2 * P)
@@ -297,7 +293,7 @@ def tile_attend_threeviews_abstaining_delivered_kernel(
             faded(late[:, e - 1, :], e)
 
         kept_t = tile("kept_t", [P, 8, 2 * P], F32, tag="laid_w1")
-        for n, b in enumerate((3, 7, 4, 5)):
+        for n, b in enumerate((3, 7, 0, 1)):
             turned = bank(b, "old_turned%d" % n)
             for k in range(2):
                 c = 2 * n + k
@@ -318,13 +314,13 @@ def tile_attend_threeviews_abstaining_delivered_kernel(
         window_t = tile("window_t", [P, 8, P], F32)
         result0 = tile("result0", [P, M], F32)
         for h in range(2):
-            turned = bank((6, 0)[h], "window_turned%d" % h)
+            turned = bank(4 + h, "window_turned%d" % h)
             for k in range(4):
                 c = 4 * h + k
                 nc.tensor.transpose(turned[:, k * P : (k + 1) * P], window[0][:, c * P : (c + 1) * P], ident[:])
             nc.scalar.copy(window_t[:, 4 * h : 4 * h + 4, :], turned[:].rearrange("p (k e) -> p k e", k=4))
         for h in range(2):
-            summed_back = bank(1 + h, "result_back%d" % h)
+            summed_back = bank((6, 2)[h], "result_back%d" % h)
             for k in range(4):
                 c = 4 * h + k
                 dst = summed_back[:, k * P : (k + 1) * P]

from contextlib import ExitStack

import concourse.mybir as mybir
from concourse.masks import make_identity

F32 = mybir.dt.float32
BF16 = mybir.dt.bfloat16
I32 = mybir.dt.int32
U32 = mybir.dt.uint32
U16 = mybir.dt.uint16
U8 = mybir.dt.uint8
FP8X4 = mybir.dt.float8_e4m3fn_x4
ALU = mybir.AluOpType
ACT = mybir.ActivationFunctionType
AX = mybir.AxisListType

P = 128
PACK = 4
D, T, I, Q, E, M = 512, 2048, 512, 512, 512, 1024
FLOPS = 4 * 2 * 512 * 512 * 512


def tile_attend_threeviews_abstaining_delivered_kernel(
    tc, query, query2, query3, keys_words, keys_scales, eager, thresh, qs, msgs, old, fade, offs, offs2, out
):
    nc = tc.nc
    with ExitStack() as ctx:
        lists = ctx.enter_context(tc.tile_pool(name="lists", bufs=1))
        sb = ctx.enter_context(tc.tile_pool(name="sb", bufs=1))
        ps = ctx.enter_context(tc.psum_pool(name="ps", bufs=1))

        def tile(name, shape, dtype, tag=None):
            return sb.tile(shape, dtype, name=name, tag=tag or name, align_bytes=64)

        def bank(n, name):
            return ps.tile([P, 512], F32, name=name, tag="bank%d" % n)

        key_bytes = tile("key_bytes", [P, T], U8)
        nc.vector.memset(key_bytes[:].bitcast(I32), 0)
        warm = tile("warm", [P, 1], F32)
        nc.gpsimd.memset(warm[:], 0.0)
        fade_cols = tile("fade_cols", [P, 8], F32)
        nc.sync.dma_start(fade_cols[:], fade.rearrange("o (p c) -> p (o c)", c=8))
        key_words = tile("key_words", [P, T], U32)
        nc.sync.dma_start(key_words[:].bitcast(I32), keys_words[0].rearrange("p n t -> p (n t)").bitcast(I32))
        key_list = lists.tile([P, I // 16], U16, name="key_list")
        nc.sync.dma_start(key_list[:], offs)
        warmed = tile("warmed", [P, 1], F32)
        nc.scalar.activation(warmed[:], warm[:], ACT.Exp)
        for g in range(4):
            nc.sync.dma_start(
                key_bytes[32 * g : 32 * g + 4, :].bitcast(I32), keys_scales[0, 4 * g : 4 * g + 4, :].bitcast(I32)
            )
        raw = {}
        for name, src in (("b", query2), ("c", query3), ("a", query)):
            raw[name] = tile("raw_" + name, [P, PACK, Q], F32)
            nc.sync.dma_start(raw[name][:], src.rearrange("(p j) q -> p j q", j=PACK))
        rowvec = {}
        for name, src in (("eager", eager), ("thresh", thresh), ("qs", qs)):
            rowvec[name] = tile("v_" + name, [P, PACK], F32)
            nc.sync.dma_start(rowvec[name][:], src.rearrange("(p r) o -> p (r o)", r=PACK))
        old_sb = [tile("old%d" % e, [P, M], F32) for e in range(4)]
        raw_m = tile("raw_m", [P, PACK, E], F32)
        nc.sync.dma_start(raw_m[:], msgs.rearrange("(p r) e -> p r e", r=PACK))
        for e in range(4):
            nc.sync.dma_start(old_sb[e][:], old[e * P : (e + 1) * P, :])
        col_list = lists.tile([P, I // 16], U16, name="col_list")
        nc.sync.dma_start(col_list[:], offs2)

        window = [tile("window%d" % e, [P, M], F32) for e in range(4)]
        for e in range(4):
            nc.vector.memset(window[e][:], 0.0)
        ident = tile("ident", [P, P], F32)
        make_identity(nc, ident[:])
        fade_row = tile("fade_row", [P, P, 8], F32)
        for h in range(2):
            spread = bank(2 + h, "spread%d" % h)
            for c in range(4):
                col = 4 * h + c
                nc.tensor.transpose(
                    spread[:, c * P : (c + 1) * P], fade_cols[:, col : col + 1].to_broadcast([P, P]), ident[:]
                )
            nc.scalar.copy(fade_row[:, :, 4 * h : 4 * h + 4], spread[:].rearrange("p (c n) -> p n c", c=4))

        fade_flat = fade_row[:].rearrange("p n c -> p (n c)")
        fade_part = tile("fade_part", [P, 8], F32)
        for h in range(2):
            turned = bank(h, "fade_turned%d" % h)
            for c in range(4):
                col = 4 * h + c
                nc.tensor.transpose(turned[:, c * P : (c + 1) * P], fade_flat[:, col * P : (col + 1) * P], ident[:])
            nc.scalar.copy(fade_part[:, 4 * h : 4 * h + 4], turned[:, 0:512:P])

        kw = tile("kw", [P, I], U32)
        nc.vector.tensor_copy(kw[:], key_words[:].indirect(key_list[:]))
        kb = tile("kb", [P, I], U8)
        nc.vector.tensor_copy(kb[:], key_bytes[:].indirect(key_list[:]))

        def lay_pair(name, h, sign):
            laid = tile("laid_%s%d" % (name, h), [P, 2, P, PACK], BF16)
            dst = laid[:].rearrange("p t m j -> p m t j")
            src = raw[name][:].rearrange("p j (m t) -> p m t j", t=PACK)[:, :, 2 * h : 2 * h + 2, :]
            if h == 0 and sign == 1.0:
                nc.vector.tensor_copy(dst, src)
            elif h == 0:
                nc.vector.tensor_scalar(dst, src, sign, None, ALU.mult)
            else:
                nc.scalar.activation(dst, src, ACT.Copy, scale=sign)
            return laid[:].rearrange("p t m j -> p (t m j)")

        def quantise(name, laid, width, tag=None):
            words = tile("w_" + name, [P, width], U32, tag=tag)
            scales = tile("s_" + name, [P, width], U8)
            nc.vector.quantize_mx(words[:].bitcast(FP8X4), scales[:], laid)
            return words, scales

        def score(dst, operand, r, start, stop):
            words, scales = operand[r // 2]
            cols = slice((r % 2) * P, (r % 2 + 1) * P)
            nc.tensor.matmul_mx(
                dst[:], lhsT=words[:, cols].bitcast(FP8X4), lhsT_scale=scales[:, cols],
                rhs=kw[:].bitcast(FP8X4), rhs_scale=kb[:], start=start, stop=stop,
            )

        diff = [bank(r, "diff%d" % r) for r in range(4)]
        laid_b = [lay_pair("b", h, 1.0) for h in range(2)]
        qb = []
        for h in range(2):
            qb.append(quantise("b%d" % h, laid_b[h], 2 * P))
            for r in (2 * h, 2 * h + 1):
                score(diff[r], qb, r, True, False)
        laid_c = [lay_pair("c", h, -1.0) for h in range(2)]
        qc = []
        th = [tile("th%d" % r, [P, I], F32) for r in range(4)]
        for h in range(2):
            qc.append(quantise("c%d" % h, laid_c[h], 2 * P))
            for r in (2 * h, 2 * h + 1):
                score(diff[r], qc, r, False, True)
        for r in range(2):
            nc.scalar.activation(th[r][:], diff[r][:], ACT.Tanh, scale=0.5)
        laid_a = [lay_pair("a", h, 1.0) for h in range(2)]
        for r in range(2, 4):
            nc.scalar.activation(th[r][:], diff[r][:], ACT.Tanh, scale=0.5)
        qa = []
        a_ps = []
        a_words = tile("w_a0", [P, 2 * P], U32)
        a_scales = tile("s_a0", [P, 2 * P], U8)
        qa.append((a_words, a_scales))
        neg_b3 = []

        def score_a(r, n):
            a_ps.append(bank(n, "a%d" % r))
            score(a_ps[r], qa, r, True, True)

        def score_b3(r, n):
            neg_b3.append(bank(n, "negb3_%d" % r))
            score(neg_b3[r], qc, r, True, True)

        for r in range(2):
            cols = slice(r * P, (r + 1) * P)
            nc.vector.quantize_mx(
                a_words[:, cols].bitcast(FP8X4), a_scales[:, cols], laid_a[0][:, r * 512 : (r + 1) * 512]
            )
            score_a(r, 6 + r)
        score_b3(0, 0)
        score_b3(1, 1)

        row_consts = tile("row_consts", [P, 4, PACK], F32, tag="laid_a0")
        terms = (("eager", 0.5 / I), ("thresh", -0.5), ("eager", -0.5), ("qs", 0.5))
        for n, (name, times) in enumerate(terms):
            nc.gpsimd.tensor_scalar(row_consts[:, n, :], rowvec[name][:], times, 0.0, ALU.mult, ALU.add)
        mean_gain, neg_half_thresh, max_gain, half_qs = [row_consts[:, n, :] for n in range(4)]

        u = [tile("u%d" % r, [P, I], F32) for r in range(4)]
        neg_s = [tile("neg_s%d" % r, [P, I], F32) for r in range(4)]
        p = [tile("p%d" % r, [P, I], F32) for r in range(4)]
        wq = tile("wq", [P, PACK, I], BF16)

        def stat(name):
            return [tile("%s%d" % (name, r), [P, 1], F32) for r in range(4)]

        neg_sum, neg_max, p_sum, inv_sum = stat("neg_sum"), stat("neg_max"), stat("p_sum"), stat("inv_sum")
        gate_bias, gate_tanh, gate_qs, factor = stat("gate_bias"), stat("gate_tanh"), stat("gate_qs"), {r: tile("factor%d" % r, [P, 1], F32) for r in (3,)}

        def gated(r):
            nc.vector.scalar_tensor_tensor(u[r][:], th[r][:], 1.0, a_ps[r][:], ALU.add, ALU.mult)

        def summed(r):
            nc.vector.scalar_tensor_tensor(
                neg_s[r][:], u[r][:], -0.5, neg_b3[r][:], ALU.mult, ALU.add, accum_out=neg_sum[r][:]
            )
            nc.scalar.activation(
                gate_bias[r][:], neg_sum[r][:], ACT.Identity,
                scale=mean_gain[:, r : r + 1], bias=neg_half_thresh[:, r : r + 1],
            )

        def weigh(r):
            nc.vector.tensor_reduce(neg_max[r][:], neg_s[r][:], AX.X, ALU.min)
            nc.scalar.activation(
                gate_tanh[r][:], neg_max[r][:], ACT.Tanh, scale=max_gain[:, r : r + 1], bias=gate_bias[r][:]
            )
            nc.scalar.activation(
                p[r][:], neg_s[r][:], ACT.Exp, scale=-1.0, bias=neg_max[r][:], accum_out=p_sum[r][:]
            )
            nc.scalar.activation(
                gate_qs[r][:], gate_tanh[r][:], ACT.Identity,
                scale=half_qs[:, r : r + 1], bias=half_qs[:, r : r + 1],
            )

        def finish(r, first):
            nc.vector.reciprocal(inv_sum[r][:], p_sum[r][:])
            if r < 3:
                (nc.vector if r == 2 else nc.gpsimd).tensor_scalar(wq[:, r, :], p[r][:], inv_sum[r][:], gate_qs[r][:], ALU.mult, ALU.mult)
                return
            if first:
                for lo in range(0, first, P):
                    nc.vector.tensor_scalar(
                        wq[:, r, lo : lo + P], p[r][:, lo : lo + P], inv_sum[r][:], gate_qs[r][:], ALU.mult, ALU.mult
                    )
            nc.scalar.activation(factor[r][:], inv_sum[r][:], ACT.Copy, scale=gate_qs[r][:])
            nc.scalar.activation(wq[:, r, first:], p[r][:, first:], ACT.Copy, scale=factor[r][:])

        def faded(dst, e):
            for h in range(2):
                cols = slice(h * 512, (h + 1) * 512)
                nc.gpsimd.tensor_tensor(dst[:, cols], old_sb[e][:, cols], fade_flat[:, cols], ALU.mult)

        m_src = raw_m[:].rearrange("p r e -> p e r")
        gated(0)
        qa.append(quantise("a1", laid_a[1], 2 * P, tag="th0"))
        score_a(2, 2)
        score_a(3, 3)
        score_b3(2, 6)
        laid_m = [tile("laid_m0", [P, 2 * P, PACK], BF16, tag="laid_a1"), tile("laid_m1", [P, 2 * P, PACK], BF16)]
        nc.gpsimd.tensor_scalar(laid_m[0][:], m_src[:, : 2 * P, :], 1.0, 0.0, ALU.mult, ALU.add)
        gated(1)
        score_b3(3, 7)
        summed(0)
        gated(2)
        weigh(0)
        summed(1)
        gated(3)
        weigh(1)
        finish(0, 0)
        nc.scalar.copy(laid_m[1][:], m_src[:, 2 * P :, :])
        summed(2)
        summed(3)
        finish(1, 0)
        weigh(2)
        weigh(3)
        finish(2, 0)
        qm = [
            quantise("m%d" % h, laid_m[h][:].rearrange("p e r -> p (e r)"), 2 * P, tag=("neg_s1", "neg_s2")[h])
            for h in range(2)
        ]
        finish(3, 2 * P)

        w_src = wq[:].rearrange("p r i -> p i r")
        pieces = ((0, P), (P, 2 * P), (2 * P, I))
        laid_w = [tile("laid_w%d" % n, [P, hi - lo, PACK], BF16) for n, (lo, hi) in enumerate(pieces)]
        nc.vector.tensor_copy(laid_w[0][:], w_src[:, 0:P, :])
        nc.vector.tensor_copy(laid_w[1][:], w_src[:, P : 2 * P, :])
        nc.scalar.copy(laid_w[2][:], w_src[:, 2 * P :, :])
        w_words = tile("w_words", [P, I], U32)
        w_scales = tile("w_scales", [P, I], U8)
        dl = [tile("dl%d" % e, [P, I], F32) for e in range(4)]

        def deliver(dst, e, lo, hi):
            words, scales = qm[e // 2]
            cols = slice((e % 2) * P, (e % 2 + 1) * P)
            nc.tensor.matmul_mx(
                dst[:, lo:hi], lhsT=words[:, cols].bitcast(FP8X4), lhsT_scale=scales[:, cols],
                rhs=w_words[:, lo:hi].bitcast(FP8X4), rhs_scale=w_scales[:, lo:hi], start=True, stop=True,
            )

        def scatter(e, lo, hi):
            nc.vector.tensor_copy(window[e][:].indirect(col_list[:, lo // 16 : hi // 16]), dl[e][:, lo:hi])

        for n, (lo, hi) in enumerate(pieces):
            nc.vector.quantize_mx(
                w_words[:, lo:hi].bitcast(FP8X4), w_scales[:, lo:hi], laid_w[n][:].rearrange("p i r -> p (i r)")
            )
            part = bank((4, 5, 6)[n], "dl_part%d" % n)
            deliver(part, 0, lo, hi)
            nc.scalar.copy(dl[0][:, lo:hi], part[:, lo:hi])
        for e, n in ((1, 0), (2, 1), (3, 2)):
            whole = bank(n, "dl_whole%d" % e)
            deliver(whole, e, 0, I)
            nc.scalar.copy(dl[e][:], whole[:])

        late = tile("late", [P, 2, M], F32, tag="laid_w2")
        for e in (1, 2):
            faded(late[:, e - 1, :], e)

        kept_t = tile("kept_t", [P, 8, 2 * P], F32, tag="laid_w1")
        for n, b in enumerate((3, 7, 0, 1)):
            turned = bank(b, "old_turned%d" % n)
            for k in range(2):
                c = 2 * n + k
                for slot, e in enumerate((0, 3)):
                    lo = (2 * k + slot) * P
                    nc.tensor.transpose(turned[:, lo : lo + P], old_sb[e][:, c * P : (c + 1) * P], ident[:])
            for k in range(2):
                c = 2 * n + k
                nc.scalar.activation(
                    kept_t[:, c, :], turned[:, 2 * k * P : 2 * (k + 1) * P], ACT.Copy, scale=fade_part[:, c : c + 1]
                )

        def store(e, h, src, queue):
            queue.dma_start(out[e * P : (e + 1) * P, h * 512 : (h + 1) * 512], src)

        for lo, hi in pieces:
            scatter(0, lo, hi)
        window_t = tile("window_t", [P, 8, P], F32)
        result0 = tile("result0", [P, M], F32)
        for h in range(2):
            turned = bank(4 + h, "window_turned%d" % h)
            for k in range(4):
                c = 4 * h + k
                nc.tensor.transpose(turned[:, k * P : (k + 1) * P], window[0][:, c * P : (c + 1) * P], ident[:])
            nc.scalar.copy(window_t[:, 4 * h : 4 * h + 4, :], turned[:].rearrange("p (k e) -> p k e", k=4))
        for h in range(2):
            summed_back = bank((6, 2)[h], "result_back%d" % h)
            for k in range(4):
                c = 4 * h + k
                dst = summed_back[:, k * P : (k + 1) * P]
                nc.tensor.matmul(dst, kept_t[:, c, :P], ident[:], start=True, stop=False, is_transpose=True)
                nc.tensor.matmul(dst, window_t[:, c, :], ident[:], start=False, stop=True, is_transpose=True)
            nc.scalar.copy(result0[:, h * 512 : (h + 1) * 512], summed_back[:])
            store(0, h, result0[:, h * 512 : (h + 1) * 512], nc.scalar)
        kept3 = []
        for h in range(2):
            back = bank((3, 7)[h], "kept_back%d" % h)
            for k in range(4):
                nc.tensor.transpose(back[:, k * P : (k + 1) * P], kept_t[:, 4 * h + k, P:], ident[:])
            kept3.append(back)
        for e in (1, 2):
            scatter(e, 0, I)
            for h in range(2):
                cols = slice(h * 512, (h + 1) * 512)
                nc.gpsimd.tensor_tensor(late[:, e - 1, cols], late[:, e - 1, cols], window[e][:, cols], ALU.add)
                store(e, h, late[:, e - 1, cols], nc.sync)
        scatter(3, 0, I)
        result3 = tile("result3", [P, M], F32, tag="result0")
        for lo, hi, queue in ((0, 512, nc.sync), (512, 768, nc.scalar), (768, M, nc.sync)):
            h = lo // 512
            nc.vector.tensor_tensor(
                result3[:, lo:hi], window[3][:, lo:hi], kept3[h][:, lo - 512 * h : hi - 512 * h], ALU.add
            )
            queue.dma_start(out[3 * P :, lo:hi], result3[:, lo:hi])
